import numpy as np, ml_dtypes
CORES = [40,41,42,43,44,45,46,47]
N = 8
BF = ml_dtypes.bfloat16
P, T, WR, H, VIS, MT, LP = 4096, 1536, 128, 1024, 3, 2, 12
lev = np.arange(16)[:, None]
def parts(rng, step=2):
    p = np.arange(P); bit = 1 << np.maximum(LP - 1 - lev, 0); base = rng.integers(1, 3, (1, 8, 16, 1)); s = []
    for n in (P, T):
        flip = rng.random((N, 8, 16, n), dtype=np.float32) < rng.choice(np.array([0.02, 0.1, 0.3]), (N, 8, 1, n))
        s.append(np.where(flip, 3 - base, base))
    b, a = s; tree = 1 + ((p[None, :] & bit) > 0).astype(np.int64)
    start = rng.integers(0, P, (N, len(range(0, 8, step)), T))
    b[:, ::step] = np.where(lev < LP, tree, b[:, ::step])
    a[:, ::step] = np.where(lev < LP, np.moveaxis(tree[:, start], 0, 2), a[:, ::step])
    u = rng.random((N, 8, 16, P)); R = np.where(rng.random((N, 8, 16, P), dtype=np.float32) < 0.5, rng.integers(0, P, (N, 8, 16, P)), (P * u * u * u).astype(np.int64))
    near = ((p[None, :] ^ bit) & -bit) | (R[:, ::step] & (bit - 1))
    R[:, ::step] = np.where(lev < LP, near, R[:, ::step])
    E = rng.integers(0, 16, (N, 8, 16, P)); D = rng.integers(0, 16, (N, 8, 16, T))
    return b, E, R, a, D, rng.integers(0, 256, (N, 8, 16, 1)), rng.integers(60, 111, (N, 8, 16, 1))
def cut(s, n, h):
    return np.where((lev < n) & (lev != h), s, 0)
def cuts(rng, b, a):
    nb = np.maximum(rng.integers(0, 17, (N, 8, 1, P)), rng.integers(0, 17, (N, 8, 1, P))); na = rng.integers(0, 17, (N, 8, 1, T))
    nb[:, 1::2] = 4 * rng.integers(0, 5, (N, 4, 1, P)); na[:, 1::2] = 4 * rng.integers(0, 5, (N, 4, 1, T))
    return cut(b, nb, rng.integers(0, 32, (N, 8, 1, P))), cut(a, na, rng.integers(0, 24, (N, 8, 1, T)))
def pack(b, E, R, a, D, w, t):
    return {"peers": np.ascontiguousarray((b + 4 * E + 64 * R).reshape(N, 128, P)).astype(np.int32), "trav": np.ascontiguousarray((a + 4 * D).reshape(N, 128, T)).astype(np.float32).astype(BF),
            "wts": np.ascontiguousarray(w.reshape(N, 128, 1)).astype(np.int32), "th": np.ascontiguousarray(t.reshape(N, 128, 1)).astype(np.int32)}
def setup_inputs(rng):
    b, E, R, a, D, w, t = parts(rng); b, a = cuts(rng, b, a)
    return pack(b, E, R, a, D, w, t)
def setup_inputs_alone(rng):
    b, E, R, a, D, w, t = parts(rng)
    full = b[:, 1::4, :, 0].copy(); b, a = cuts(rng, b, a); b[:, 1::4, :, 0] = full
    w[:, ::2] = 0; w[:, ::2, 0] = 1; w[:, ::2, 1] = 16; t[:, ::2] = 241
    for q in range(N):
        for g in range(0, 8, 2):
            x = np.concatenate([rng.permutation(256) for i in range(T // 256)])
            D[q, g, 0] = x & 15; D[q, g, 1] = x >> 4; R[q, g] = rng.permutation(P)[None, :]
    three = rng.integers(0, 16, (N, 4, 16, 3)); D[:, 1::2] = np.take_along_axis(three, rng.integers(0, 3, (N, 4, 1, T)), 3)
    w[:, 1::4] = 0; R[:, 3::4] = rng.choice(np.array([0, P - 1, 5, P // 2]), (N, 2, 16, P))
    return pack(b, E, R, a, D, w, t)
def setup_inputs_ties(rng):
    b, E, R, a, D, w, t = parts(rng)
    b = cut(b, rng.integers(0, 3, (N, 8, 1, P)), 99); a = cut(a, rng.integers(0, 3, (N, 8, 1, T)), 99)
    v = rng.integers(1, 15, (8, 16)); o = np.argsort(rng.random((N, 8, 16, T)), axis=2)
    D = np.take_along_axis(v[None, :, :, None], o, 2)
    D = D + (lev == rng.integers(0, 16, (N, 8, 1, T))) * rng.integers(-1, 2, (N, 8, 1, T))
    E[:, ::2] = 0; E[:, 1::2] = 15; s = np.add.reduce(v, axis=1)
    t[:] = np.where(np.arange(8) % 2 == 0, s, 240 - s)[None, :, None, None]
    return pack(b, E, R, a, D, w, t)
def setup_inputs_ends(rng):
    b, E, R, a, D, w, t = parts(rng); b, a = cuts(rng, b, a); o = rng.permutation(8); base = rng.integers(1, 3, (16, 1))
    for i in (0, 1, 4, 5): a[:, o[i]] = base
    for i in (0, 1, 4, 5, 6): b[:, o[i]] = base
    a[:, o[1]] = np.where(lev == 15, rng.integers(0, 3, (N, 1, T)), base); b[:, o[1]] = np.where(lev == 15, rng.integers(0, 3, (N, 1, P)), base)
    a[:, o[2:4]] = 0; b[:, o[2:4]] = 0
    b[:, o[4]] = np.where(lev == 0, 3 - base, base); b[:, o[5]] = np.where(lev == 15, 0, base)
    a[:, o[6]] = np.where(lev == 0, 0, base); b[:, o[6]] = np.where(lev == 0, rng.integers(1, 3, (N, 1, P)), base)
    R[:, o[:4]] = np.where(rng.random((N, 4, 16, P)) < 0.5, R[:, o[:4]], rng.choice(np.array([0, P - 1]), (N, 4, 16, P)))
    x = np.stack([np.concatenate([rng.permutation(256) for i in range(T // 256)]) for q in range(2 * N)]).reshape(2, N, 1, T); z = np.arange(256)[None, :]
    h, k, n = int(o[2]), int(o[3]), int(o[7]); v = rng.integers(0, 16, (16, 1)); sh = np.minimum(lev, 7)
    t[:, h] = 0; w[:, h] = np.where(lev == 0, 1, np.where(lev == 1, 16, 0))
    D[:, h] = np.where(lev == 0, x[0] & 15, np.where(lev == 1, x[0] >> 4, v)); E[:, h, :, :256] = np.where(lev == 0, z & 15, np.where(lev == 1, z >> 4, v))
    t[::2, k] = 241; t[1::2, k] = 240; w[:, k] = np.where(lev < 8, 1 << sh, 0)
    D[:, k] = 15 * np.where(lev < 8, (x[1] >> sh) & 1, 1)
    there = E[:, k]; there[:, :, (15 * z[0]) & (P - 1)] = 15 - 15 * np.where(lev < 8, (z >> sh) & 1, 1)
    w[:, n] = rng.integers(240, 256, (N, 16, 1)); D[:, n] = rng.integers(13, 16, (N, 16, T))
    return pack(b, E, R, a, D, w, t)
def setup_inputs_grid(rng):
    b, E, R, a, D, w, t = parts(rng, 1); p = np.arange(P)[None, :]
    b = cut(b, 16, rng.integers(0, 64, (N, 8, 1, P))); a = cut(a, rng.integers(6, 17, (N, 8, 1, T)), rng.integers(0, 5, (N, 8, 1, T)))
    late = (lev >= 12) & (lev < 15); bit = 1 << np.clip(lev - 12, 0, 2); low = (p & (bit - 1)) | ((p ^ bit) & bit)
    for i in rng.permutation(8)[:2]:
        g = int(i); base = rng.integers(1, 3, (16, 1))
        b[:, g] = np.where(lev == 15, rng.integers(1, 3, (N, 1, P)), np.where(late & ((p & bit) > 0), 3 - base, base))
        hole = (lev == rng.integers(12, 15, (N, 1, T))) | (lev == rng.choice(np.array([12, 13, 14, 99, 99, 99]), (N, 1, T)))
        a[:, g] = np.where(hole, 0, np.where(lev == 15, rng.integers(1, 3, (N, 1, T)), base))
        R[:, g] = np.where(late, (R[:, g] & -8) | low, R[:, g])
    return pack(b, E, R, a, D, w, t)
def setup_inputs_spread(rng):
    b, E, R, a, D, w, t = parts(rng)
    u = rng.random((N, 8, 1, P)); b = np.where(rng.random((N, 8, 16, P)) < u * u, 0, b)
    u = rng.random((N, 8, 1, T)); a = np.where(rng.random((N, 8, 16, T)) < u * u, 0, a)
    u = rng.random((N, 8, 1, P)); E = (16 * rng.random((N, 8, 16, P)) * u * u).astype(np.int64)
    u = rng.random((N, 8, 1, T)); D = (16 * rng.random((N, 8, 16, T)) * u * u).astype(np.int64)
    R = np.minimum(np.exp2(LP * rng.random((N, 8, 16, P))).astype(np.int64), P) - 1; R[:, 1::2] = P - 1 - R[:, 1::2]
    w = np.minimum(np.exp2(8 * rng.random((N, 8, 16, 1))).astype(np.int64), 255) * (rng.random((N, 8, 16, 1)) > 0.125)
    return pack(b, E, R, a, D, w, rng.integers(0, 242, (N, 8, 16, 1)))
def check_inputs(d):
    bad = []
    for k, hi in (("peers", 64 * P - 1), ("wts", 255), ("th", 241)):
        if np.min(d[k]) < 0 or np.max(d[k]) > hi: bad.append("range of " + k)
    if np.any((np.asarray(d["peers"]).astype(np.int64) & 3) == 3): bad.append("symbols of peers")
    t = np.asarray(d["trav"]).astype(np.float64)
    if not np.all((t >= 0) & (t <= 62) & (t == np.floor(t))): bad.append("range of trav")
    if np.any(t - 4 * np.floor(t * 0.25) == 3): bad.append("symbols of trav")
    return bad
def reference(peers, trav, wts, th):
    c = peers.astype(np.int32).reshape(N, 8, 16, P); B = c & 3; E = (c >> 2) & 15; R = c >> 6
    t = trav.astype(np.float32).astype(np.int32).reshape(N, 8, 16, T); a = t & 3; D = t >> 2
    w = wts.astype(np.int32).reshape(N, 8, 16, 1); lim = th.astype(np.int32).reshape(N, 8, 16, 1)
    below = np.arange(WR)[None, :] < np.arange(WR)[:, None]
    for visit in range(VIS):
        if visit: a = np.roll(a, 1, axis=0); D = np.roll(D, 1, axis=0)
        G = np.full(a.shape, -1, np.int32)
        m = (np.add.reduce(w * D, axis=2) & (P - 1)).astype(np.int64)
        for meeting in range(MT):
            ix = m[:, :, None, :]
            b = np.take_along_axis(B, ix, 3); e = np.take_along_axis(E, ix, 3); r = np.take_along_axis(R, ix, 3)
            part = (a != b) | (a == 0) | (b == 0)
            l = np.where(np.any(part, axis=2), np.argmax(part, axis=2), 15)[:, :, None, :]
            at = lev == l
            al = np.take_along_axis(a, l, 2); bl = np.take_along_axis(b, l, 2); rl = np.take_along_axis(r, l, 2); tl = np.take_along_axis(lim, l, 2)
            far = np.add.reduce(np.abs(D - e), axis=2)[:, :, None, :]
            s = m[:, :, :WR]; twin = np.any((s[..., :, None] == s[..., None, :]) & below, axis=3)
            wr = np.zeros((N, 8, T), bool); wr[:, :, :WR] = ~twin; wl = wr[:, :, None, :]
            c1 = wl & (al == 0) & (bl == 0) & (far >= tl); c2 = (al == 0) & (bl != 0)
            c3 = wl & (al != 0) & (bl == 0); c4 = wl & (al != 0) & (bl != 0) & (al != bl)
            swap = c4 & (lev < l) & (G >= 0)
            na = np.where(at & c1, 1, np.where(at & c2, 3 - b, a)).astype(np.int32)
            nb = np.where(at & c1, 2, np.where(at & c3, 3 - a, b)).astype(np.int32)
            nd = np.where(c1, np.maximum(D, e), D); ne = np.where(c1, np.minimum(D, e), e)
            nr = np.where((at & c3 & (G >= 0)) | swap, G, r)
            ng = np.where(at & (c1 | c2), ix, np.where(swap, r, G)).astype(np.int32)
            for q in range(N):
                for g in range(8):
                    j = np.flatnonzero(wr[q, g]); p = m[q, g, j]
                    B[q, g][:, p] = nb[q, g][:, j]; E[q, g][:, p] = ne[q, g][:, j]; R[q, g][:, p] = nr[q, g][:, j]
            a, D, G = na, nd, ng; m = rl[:, :, 0, :].astype(np.int64)
    yp = (B + 4 * E + 64 * R)[..., :H]
    return {"yp": np.ascontiguousarray(yp.reshape(N, 128, H)).astype(np.float32), "yt": np.ascontiguousarray((a + 4 * D).reshape(N, 128, T)).astype(np.float32).astype(BF)}

@@ -1,0 +1,578 @@
+import numpy as np
+from concourse.mybir import AluOpType as A, AxisListType, ActivationFunctionType as F
+
+P, NT, WR, H = 4096, 1536, 128, 1024
+NB = NT - WR
+TW = P + 240
+CH = [(0, 352), (352, 704), (704, 1056), (1056, 1408)]
+WG = [[0, 1], [2, 3]]
+LP = [0, 608, 1216, 1824, 2432, 3040, 3648, 3968, 4096]
+LC = len(LP) - 1
+HP = 3072
+SCRATCH = {
+    "TP": ("sbuf", [128, TW], "int32"), "TR": ("sbuf", [128, TW], "int32"), "TB": ("sbuf", [128, TW], "int32"),
+    "IOTA": ("sbuf", [128, P], "float32"), "eq": ("sbuf", [128, 48, 128], "bfloat16"),
+    "hb": ("sbuf", [128, 58600], "bfloat16"), "hf": ("sbuf", [128, 3300], "float32"),
+    "hi": ("sbuf", [128, 4200], "int32"), "hh": ("sbuf", [128, 5800], "float16"), "hu": ("sbuf", [128, 800], "uint16"),
+}
+for _k in range(8):
+    SCRATCH["ps%d" % _k] = ("psum", [128, 512], "float32")
+SEMAPHORES = ["pe", "dve", "act", "pool", "lsem"] + ["d%d" % _k for _k in range(24)] + ["r%d" % _k for _k in range(16)]
+ALIGN = {"hb": 8, "hf": 4, "hi": 4, "hh": 8, "hu": 8}
+CYC, GA, SC, FIX, PEC, LAT, BW = 1.0, 1.56, 3.8, 60.0, 0.5, 100.0, 200.0
+CASES = [(1, 1, 1, 100), (1, .72, .5, 60), (1, 1.28, 1.5, 200), (.8, 1, 1, 200), (1.3, 1, 1, 100)]
+TRIES, SEED, EPS = 2500, 0, 100
+RC = -(2048 + 31.0 / 64)
+PLAN = {}
+
+
+def build(g, core, T, topo):
+    ops, lastw, readers, top = [], {}, {}, {k: 0 for k in ALIGN}
+    bank = {}
+    cnt = {"d": 0, "r": 0, "t": 0}
+    n = len(T.cores)
+    rank = T.rank_of(core)
+    V, S, PE = g.vector, g.scalar, g.tensor
+
+    def tile(buf, w):
+        b = top[buf]
+        top[buf] = b + (w + ALIGN[buf] - 1) // ALIGN[buf] * ALIGN[buf]
+        assert top[buf] <= SCRATCH[buf][1][1], (buf, top[buf])
+        cnt["t"] += 1
+        return (buf, b, w, "t%d" % cnt["t"])
+
+    def sub(t, a, b, tag=None):
+        return (t[0], t[1] + a, b - a, t[3] if tag is None else "%s.%s" % (t[3], tag))
+
+    def chunks(t, o=0):
+        return [sub(t, o + s, o + e, k) for k, (s, e) in enumerate(CH)]
+
+    def ap(t, a=0, b=None, step=None):
+        if len(t) > 4:
+            return T[t[0]][:, t[1] + t[4]:t[1] + t[2]:16]
+        b = t[2] if b is None else b
+        return T[t[0]][:, t[1] + a:t[1] + b:step] if step else T[t[0]][:, t[1] + a:t[1] + b]
+
+    def nm(x):
+        return x if isinstance(x, str) else x[3]
+
+    def op(eng, cost, rd, wr, fn, ps_in=None, ps_out=None, sig=None, after=(), lat=0.0, alt=None, kind=""):
+        i = len(ops)
+        deps = set(after)
+        rd = [nm(x) for x in rd] + ([ps_in] if ps_in else [])
+        wr = [nm(x) for x in wr] + ([ps_out] if ps_out else [])
+        for x in rd:
+            deps.add(lastw[x])
+        for x in wr:
+            if x in lastw:
+                deps.add(lastw[x])
+            deps.update(readers.get(x, ()))
+        for x in rd:
+            readers.setdefault(x, []).append(i)
+        for x in wr:
+            lastw[x] = i
+            readers[x] = []
+        deps.discard(i)
+        ops.append(dict(eng=eng, cost=cost, deps=deps, fn=fn, pi=ps_in, po=ps_out, sig=sig, lat=lat, kind=kind,
+                        opts=[(eng, cost, fn)] + ([alt] if alt else [])))
+        return i
+
+    def ps(name, w, a=0):
+        return T["ps%d" % bank[name]][:, a:w]
+
+    def vc(w, c=1.0):
+        return FIX + max(64, w * c) * CYC
+
+    def mm(w, terms, more=0):
+        cnt["t"] += 1
+        name = "p%d" % cnt["t"]
+
+        def fn():
+            for k, t in enumerate(terms):
+                a, b = t[3] if len(t) > 3 else (0, w)
+                r = PE.matmul(ps(name, b, a), t[0], t[1], k == 0, k == len(terms) - 1)
+            return r
+        c = more + sum(max(64, (t[3][1] - t[3][0]) if len(t) > 3 else w) for t in terms)
+        op("pe", 30 + c * PEC, [x for t in terms for x in t[2]], [], fn, ps_out=name)
+        return name
+
+    def term(m, x):
+        return (ap(m), ap(x), [m, x])
+
+    def act(out, src, func, scale=1.0, bias=0.0, rd=(), dve=None):
+        w = out[2]
+        isp = isinstance(src, str)
+        if func == F.Identity:
+            dve = (scale, bias, A.mult, A.add)
+        if func == F.Relu:
+            dve = (bias, 0.0, A.add, A.max)
+
+        def x():
+            return ps(src, w) if isp else ap(src)
+        fast = 0.5 if not isp and src[0] == "hb" and out[0] == "hb" else 1.0
+        alt = dve and ("dve", vc(w, fast), lambda: V.tensor_scalar(ap(out), x(), *dve))
+        return op("act", vc(w), ([] if isp else [src]) + list(rd), [out],
+                  lambda: S.activation(ap(out), x(), func, bias=bias, scale=scale), ps_in=src if isp else None, alt=alt)
+
+    def ts(out, src, s1, s2, *o):
+        return op("dve", vc(out[2]), [src], [out], lambda: V.tensor_scalar(ap(out), ap(src), s1, s2, *o))
+
+    def tt(out, x, y, o):
+        w = out[2]
+        if isinstance(x, str):
+            return op("dve", vc(w), [y], [out], lambda: V.tensor_tensor(ap(out), ps(x, w), ap(y), o), ps_in=x)
+        return op("dve", vc(w, 2), [x, y], [out], lambda: V.tensor_tensor(ap(out), ap(x), ap(y), o))
+
+    def cp(out, src):
+        return op("dve", vc(out[2]), [src], [out], lambda: V.tensor_copy(ap(out), ap(src)))
+
+    def parts(tab):
+        return ["%s%d" % (tab, k) for k in range(2 if tab == "IOTA" else LC)]
+
+    def ind(tab, off, w=P):
+        return T[tab][:, 0:w].indirect(ap(off))
+
+    def gact(out, tab, off, func, scale, bias):
+        c = vc(out[2], GA)
+        return op("act", c, parts(tab) + [off], [out],
+                  lambda: S.activation(ap(out), ind(tab, off), func, bias=bias, scale=scale), kind="g",
+                  alt=func == F.Identity and ("dve", c, lambda: V.tensor_scalar(ap(out), ind(tab, off), scale, bias, A.mult, A.add)))
+
+    def gtt(out, tab, off, y, o):
+        return op("dve", vc(out[2], GA), parts(tab) + [off, y], [out], lambda: V.tensor_tensor(ap(out), ind(tab, off), ap(y), o), kind="g")
+
+    def scat(tab, off, src):
+        return op("dve", vc(src[2], SC), [off, src], parts(tab), lambda: V.tensor_copy(ind(tab, off, TW), ap(src)), kind="s")
+
+    def dma(out, in_, rd, wr, nbytes):
+        s = "d%d" % cnt["d"]
+        cnt["d"] += 1
+        return op("sync", 60.0, rd, wr, lambda: g.sync.dma_start(out, in_), sig=(s, 16), lat=nbytes, kind="" if rd else "load")
+
+    def send(src, dst, hop, rd, after=()):
+        s = "r%d" % cnt["r"]
+        cnt["r"] += 1
+        to = T.cores[(rank + hop) % n]
+        ne = len(topo.engines(T.cores[(rank - hop) % n], core))
+        rid, pid, _ = topo.addr(to)
+        i = op("pool", 400.0, rd, [], lambda: g.remote_dma(ap(dst), ap(src), T.sem[s], T.sem.lsem, pid, rid, topo.mask(core, to)),
+               sig=("lsem", len(topo.engines(core, to))), lat=src[2] * 256, after=after)
+        return op("recv", 0.0, [], [dst], None, sig=(s, ne), after=[i])
+
+    def B(w=128):
+        return tile("hb", w)
+
+    wi, thi = tile("hi", 1), tile("hi", 1)
+    trav = B(NT)
+    tw0, tb0 = sub(trav, 0, WR, "w"), sub(trav, WR, NT, "b")
+    dma(ap(wi), T.wts[:], [], [wi], 512)
+    dma(ap(thi), T.th[:], [], [thi], 512)
+    for k in range(LC):
+        dma(T.TP[:, LP[k]:LP[k + 1]], T.peers[:, LP[k]:LP[k + 1]], [], ["TP%d" % k], (LP[k + 1] - LP[k]) * 512)
+        if k == 0:
+            dma(ap(trav), T.trav[:], [], [tw0, tb0], NT * 256)
+    last_load = lastw["TP%d" % (LC - 1)]
+
+    def fill(t, val, a=0, b=None, step=None):
+        op("dve", vc(t[2] / (step or 1), 0.5), [], [t], lambda: V.memset(ap(t, a, b, step), val))
+
+    def sel(out, src, pat, cmp, f, base, cm):
+        op("pool", 170 + 2 * 128 * CYC, [src], [out], lambda: g.affine_select(ap(out), ap(src), pat, cmp, f, base, cm))
+
+    def scaled(src, s, rd=()):
+        t = B(src[2])
+        act(t, src, F.Identity, scale=s, rd=rd)
+        return t
+    ONES, C35, g1, G, I, TS = [B() for _ in range(6)]
+    fill(ONES, 1.0)
+    fill(C35, 3.5)
+    sel(I, ONES, [[-1, 128]], A.is_equal, 0.0, 0, 1)
+    sel(g1, ONES, [[-16, 8], [0, 16]], A.is_ge, 0.0, 0, 1)
+    sel(G, g1, [[16, 8], [0, 16]], A.is_ge, 0.0, 15, -1)
+    sel(TS, G, [[1, 128]], A.is_gt, 0.0, 0, -1)
+    Z = B(144)
+    fill(Z, 0.0)
+    op("dve", vc(8), [G], [Z], lambda: V.tensor_copy(ap(Z, 15, 143, 16), ap(G, 0, 128, 16)))
+    wf, cb, rs, r1, gb, ct, gt = [tile("hf", 1) for _ in range(7)]
+    ts(wf, wi, 0.25, None, A.mult)
+    Zw, Gw = scaled(Z, ap(wf), [wf]), scaled(G, ap(wf), [wf])
+    Z16, G16 = tile("hh", 144), tile("hh", 128)
+    cp(Z16, Z)
+    cp(G16, G)
+    ts(cb, thi, -1024.0, -851840.0, A.mult, A.add)
+    ts(ct, thi, 4.0, 3328.0, A.mult, A.add)
+    op("dve", vc(128), [TS], [rs], lambda: V.tensor_reduce(ap(rs), ap(TS), AxisListType.X, A.add))
+    ts(r1, rs, 0.0, 352.0, A.is_equal, A.mult)
+    ts(gb, r1, -176.0, None, A.add)
+    ts(gt, gb, -1.0 / 32, None, A.mult)
+    nI, p12I, m12I, nK, pK, I15, I25, I8K = [scaled(I, s) for s in (-1.0, 12.0, -12.0, -1024.0, 1024.0, 1.5, 2.5, 8192.0)]
+    nT64, nTK, GK = scaled(TS, -64.0), scaled(TS, -1024.0), scaled(G, 1024.0)
+    MV = B()
+    sel(MV, nT64, [[-1, 128]], A.not_equal, 11.0, 0, 1)
+    n64f = tile("hf", 128)
+    act(n64f, I, F.Identity, scale=-64.0)
+    K2, THR, GP0, GP1, Wt, W0, Wm, M1 = [B() for _ in range(8)]
+    INJ = B(144)
+    fill(K2, 0.5)
+    fill(K2, 0.0, 0, 128, 16)
+    fill(INJ, 0.0)
+    fill(INJ, -1024.0, 0, 144, 16)
+    op("dve", vc(128), [K2, INJ], [THR], lambda: V.tensor_tensor_scan(ap(THR), ap(K2), ap(INJ, 0, 128), 0.0, A.mult, A.add))
+    tt(GP0, G, THR, A.mult)
+    op("dve", vc(128), [GP0], [GP1], lambda: V.transpose(ap(GP1), ap(GP0)))
+    GP = scaled(GP1, -0.5)
+    K32 = scaled(K2, 1.0 / 16)
+    op("dve", vc(128), [K32, I], [Wt], lambda: V.tensor_tensor_scan(ap(Wt), ap(K32), ap(I), 0.0, A.mult, A.add))
+    op("dve", vc(128), [Wt], [W0], lambda: V.transpose(ap(W0), ap(Wt)))
+    sel(Wm, W0, [[-1, 128]], A.not_equal, -1.0, 0, 1)
+    tt(M1, Wm, nT64, A.add)
+    M2 = scaled(Wm, -8.0)
+    MASK, MASK6, JB = B(), B(), B()
+    act(MASK, mm(128, [(ap(Z, 15 - i, 143 - i), ap(INJ, 16 - i, 144 - i), [Z, INJ]) for i in range(16)]), F.Identity, 1.0 / 128, 128.0)
+    act(MASK6, MASK, F.Identity, 1.0, 6.0)
+    op("pool", 400.0, [], [JB], lambda: g.iota(ap(JB), [[16, 8], [0, 16]], 0, 1, allow_small_or_imprecise_dtypes=True))
+    RST = scaled(sub(INJ, 0, 128), 1024.0)
+    op("pool", 130 + 2 * HP * CYC, [], ["IOTA0"],
+       lambda: g.iota(T.IOTA[:, 0:HP], [[1, HP]], 0, 0, allow_small_or_imprecise_dtypes=True))
+    op("act", vc(P - HP), ["IOTA0"], ["IOTA1"], lambda: S.activation(T.IOTA[:, HP:P], T.IOTA[:, 0:P - HP], F.Identity, bias=float(HP), scale=1.0),
+       alt=("dve", vc(P - HP), lambda: V.tensor_scalar(T.IOTA[:, HP:P], T.IOTA[:, 0:P - HP], float(HP), None, A.add)))
+
+    for k in range(LC):
+        tp, tr, tb = [T[x][:, LP[k]:LP[k + 1]] for x in ("TP", "TR", "TB")]
+        c = vc(LP[k + 1] - LP[k])
+        op("dve", c, ["TP%d" % k], ["TB%d" % k], lambda tp=tp, tb=tb: V.tensor_scalar(tb, tp, 3, None, A.bitwise_and))
+        op("act", c, ["TP%d" % k], ["TR%d" % k], lambda tp=tp, tr=tr: S.activation(tr, tp, F.Identity, bias=RC, scale=1.0 / 64),
+           alt=("dve", c, lambda tp=tp, tr=tr: V.tensor_scalar(tr, tp, 1.0 / 64, RC, A.mult, A.add)))
+
+    def split(t, a, d4):
+        x = B(t[2])
+        act(x, t, F.Identity, scale=0.25, bias=127.75)
+        act(d4, x, F.Identity, scale=4.0, bias=-512.0)
+        for tc, ac, dc in a:
+            act(ac, mm(tc[2], [(ap(I), ap(tc), [I, t]), (ap(nI), ap(dc), [nI, d4])]), F.Identity)
+    aw, dw = B(), B()
+    split(tw0, [(tw0, aw, dw)], dw)
+    DB = [B(NB) for _ in range(3)]
+    abc = chunks(B(NB))
+    split(tb0, list(zip(chunks(tb0), abc, chunks(DB[0]))), DB[0])
+    for hop in (1, 2):
+        send(DB[0], DB[hop], hop, [DB[0]], [last_load])
+
+    def wrap(z, x, rd):
+        return mm(x[2] // 16, [(ap(z, 15 - i, 143 - i), ap(x, i, x[2], 16), [z] + rd) for i in range(16)])
+
+    def pick(terms, buf):
+        x = tile(buf, 128)
+        p = mm(128, terms)
+        op("dve", vc(128), [RST], [x], lambda: V.tensor_tensor_scan(ap(x), ap(RST), ps(p, 128), 0.0, A.add, A.max), ps_in=p)
+        return x + (15,)
+
+    def first_peer(d4, off, mw=None):
+        w = d4[2] // 16
+        y = tile("hi", w)
+        if mw:
+            x = pick([term(nK, MASK), term(Gw, d4)], "hi")
+        else:
+            x = tile("hi", w)
+            act(x, wrap(Zw, d4, [d4]), F.Identity)
+        ts(y, x, P - 1, None, A.bitwise_and)
+        cp(off, y)
+        if mw:
+            act(mw, y, F.Identity, 1.0, -2048.0)
+
+    def level(ga, nn):
+        act(ga, mm(nn[2], [term(MV, nn)]), F.Sigmoid, scale=32.0, bias=ap(gb), rd=[gb, gt], dve=(ap(gt), None, A.is_ge))
+
+    def writers(v, j, a, d4, off, mw, an, dn, prev):
+        last = v == 2 and j == 1
+        be, nn, al, ad, Eb, tw, c1, db = [B() for _ in range(8)]
+        Pg, E4, Pn = tile("hi", 128), tile("hi", 128), tile("hi", 128)
+        gact(be, "TB", off, F.Abs, 2.5, -3.25)
+        if j == 0:
+            Mb = tile("hh", 128)
+            gact(Mb, "IOTA", off, F.Identity, 1.0, -2048.0)
+        else:
+            M0, al0, se0 = prev
+            pm = mm(128, [term(G16, se0)])
+        gact(Pg, "TP", off, F.Identity, 1.0, 0.0)
+        ts(E4, Pg, 60, None, A.bitwise_and)
+        act(Eb, E4, F.Identity)
+        act(ad, mm(128, [term(nI, d4), term(I, Eb)]), F.Abs)
+        act(nn, mm(128, [term(nI, a), term(I, be)]), F.Abs, bias=0.25)
+        act(al, a, F.Abs, scale=2.5, bias=-3.25)
+        s8 = 8 * (2 * v + j)
+        en = ["eq%d" % (s8 + c) for c in range(8)]
+        for c in range(8):
+            op("dve", vc(128 - 16 * c, 1.0 if j else 0.5), [mw] + ([] if j else [Mb]), [en[c]], lambda c=c: V.tensor_scalar(
+                T.eq[:, s8 + c, 0:128 - 16 * c], ps(pm, 128, 16 * c) if j else ap(Mb, 16 * c, 128),
+                ap(mw, c, c + 1), None, A.is_equal), ps_in=pm if j else None)
+        ptw = mm(128, [term(I, THR), (ap(GP), T.eq[:, s8:s8 + 8, 0:16], [GP] + en)]
+                 + [(ap(GK), T.eq[:, s8 + c, 16:128 - 16 * c], [GK], (16 * c + 16, 128)) for c in range(7)])
+        act(tw, ptw, F.Sigmoid, scale=16384.0, bias=128.0, dve=(0.0, None, A.is_ge))
+        s1, soff = tile("hf", 8), tile("hu", 8)
+        tt(s1, pick([term(nK, MASK6), term(I, JB), term(I8K, tw)], "hf"), mw, A.max)
+        ts(soff, s1, 2048.0, None, A.add)
+        act(c1, mm(128, [term(nK, a), term(pK, be), term(G, ad), term(nTK, nn), term(nK, tw)]), F.Sigmoid,
+            scale=256.0, bias=ap(cb), rd=[cb, ct], dve=(ap(ct), None, A.is_ge))
+        out = None
+        if j == 0:
+            ga, se, off2, mw2 = B(), tile("hh", 128), tile("hu", 8), tile("hf", 8)
+            level(ga, nn)
+            gtt(se, "TR", off, ga, A.mult)
+            pw = pick([term(nK, MASK), term(G16, se)], "hf")
+            ts(off2, pw, 2048.0, None, A.add)
+            cp(mw2, pw)
+            out = (off2, mw2, (Mb, al, se))
+        tt(an, mm(128, [term(MV, nn), term(m12I, be), term(I15, c1)]), a, A.max)
+        tt(dn, mm(128, [term(I, Eb), term(nK, ONES), term(GK, c1)]), d4, A.max)
+        act(db, mm(128, [term(nI, al), term(nTK, nn), term(pK, be), term(I25, c1)]), F.Relu, bias=2.75 - 3328.0)
+        terms = [term(I, d4), term(nI, dn), term(I, db)]
+        if j == 1:
+            bad, sw, dm, sd = B(), B(), tile("hf", 128), tile("hf", 128)
+            act(bad, mm(128, [term(I, al), term(I, be)]), F.Relu, bias=-3.5)
+            act(sw, mm(128, [term(m12I, C35), term(p12I, al0), term(p12I, a), term(m12I, al), term(M1, nn), term(M2, bad)]),
+                F.Sigmoid, scale=2.0 ** 84, bias=-100.0, dve=(0.0, None, A.is_gt))
+            gtt(dm, "TR", off, M0, A.subtract)
+            tt(sd, dm, sw, A.mult)
+            terms = [term(n64f, sd)] + terms
+        tt(Pn, mm(128, terms, 384 * j), Pg, A.add)
+        if not last:
+            bn = tile("hi", 128)
+            ts(bn, Pn, 3, None, A.bitwise_and)
+            scat("TB", soff, bn)
+        scat("TP", soff, Pn)
+        if j == 1 and not last:
+            rn = tile("hi", 128)
+            act(rn, Pn, F.Identity, 1.0 / 64, RC)
+            scat("TR", soff, rn)
+        return out
+
+    def bulk_gather(offs):
+        bc = chunks(B(NB))
+        for k in range(len(CH)):
+            gact(bc[k], "TB", offs[k], F.Abs, 2.5, -3.25)
+        return bc
+
+    def bulk_rest(bc, a, an, k, extra=(), base=None):
+        nn = B(bc[k][2])
+        w = nn[2]
+        act(nn, mm(w, [term(nI, a[k]), term(I, bc[k])]), F.Abs, bias=0.25)
+        tt(an[k], mm(w, list(extra) + [term(m12I, bc[k]), term(MV, nn)]), base or a[k], A.max)
+        return nn
+
+    YT, YP = B(NT), tile("hf", H)
+    for v in range(3):
+        offw, mww = tile("hu", 8), tile("hf", 8)
+        first_peer(dw, offw, mww)
+        ob = tile("hu", NB // 16)
+        first_peer(DB[v], ob)
+        o1 = [sub(ob, s // 16, e // 16) for s, e in CH]
+        bc = bulk_gather(o1)
+        a1w, d1w = B(), B()
+        off2, mw2, prev = writers(v, 0, aw, dw, offw, mww, a1w, d1w, None)
+        a1c = chunks(B(NB))
+        se = tile("hh", NB)
+        sec = chunks(se)
+        t1 = chunks(B(NB)) if v == 2 else None
+        for k, (s, e) in enumerate(CH):
+            ga = B(e - s)
+            level(ga, bulk_rest(bc, abc, a1c, k))
+            gtt(sec[k], "TR", o1[k], ga, A.mult)
+            if v == 2:
+                act(t1[k], mm(e - s, [(ap(I), ap(DB[v], s, e), [DB[v]]), term(I, a1c[k])]), F.Identity)
+        o2 = {}
+        for grp in WG:
+            s, e = CH[grp[0]][0], CH[grp[-1]][1]
+            o = tile("hu", (e - s) // 16)
+            p = wrap(Z16, sub(se, s, e), [sec[k] for k in grp])
+            op("dve", vc(o[2]), [], [o], lambda o=o, p=p: V.tensor_scalar(ap(o), ps(p, o[2]), 2048.0, None, A.add), ps_in=p)
+            for k in grp:
+                o2[k] = sub(o, (CH[k][0] - s) // 16, (CH[k][1] - s) // 16)
+        bc = bulk_gather(o2)
+        ws = B(256)
+        a2w, d2w = sub(ws, 0, 128, "a"), sub(ws, 128, 256, "d")
+        writers(v, 1, a1w, d1w, off2, mw2, a2w, d2w, prev)
+        if v < 2:
+            land = B(256)
+            send(ws, land, 1, [a2w, d2w])
+            aw, dw = sub(land, 0, 128), sub(land, 128, 256)
+            a2c, abc = chunks(B(NB)), chunks(B(NB))
+            for k in range(len(CH)):
+                bulk_rest(bc, a1c, a2c, k)
+                send(a2c[k], abc[k], 1, [a2c[k]])
+        else:
+            y = sub(YT, 0, WR, "w")
+            tt(y, a2w, d2w, A.add)
+            yc = chunks(YT, WR)
+            for k, (s, e) in enumerate(CH):
+                bulk_rest(bc, a1c, yc, k, [(ap(I), ap(DB[v], s, e), [DB[v]])], t1[k])
+                dma(T.yt[:, WR + s:WR + e], ap(yc[k]), [yc[k]], [], (e - s) * 256)
+            dma(T.yt[:, 0:WR], ap(y), [y], [], WR * 256)
+            for k in range(2):
+                a, b = k * H // 2, (k + 1) * H // 2
+                yk = sub(YP, a, b, k)
+                op("dve", vc(H // 2), parts("TP"), [yk], lambda a=a, b=b, yk=yk: V.tensor_copy(ap(yk), T.TP[:, a:b]),
+                   alt=("act", vc(H // 2), lambda a=a, b=b, yk=yk: S.activation(ap(yk), T.TP[:, a:b], F.Identity)))
+                dma(T.yp[:, a:b], ap(yk), [yk], [], H * 256)
+    PLAN["top"], PLAN["ops"] = top, ops
+    return ops, bank
+
+
+def dma_end(o, end, free):
+    free[0] = max(free[0], end + 1300) + o["lat"] / BW
+    return free[0] + 500
+
+
+def schedule(ops, noise, bias, eps):
+    n = len(ops)
+    succ = [[] for _ in ops]
+    for i, o in enumerate(ops):
+        for d in o["deps"]:
+            succ[d].append(i)
+    prio = [0.0] * n
+    for i in range(n - 1, -1, -1):
+        o = ops[i]
+        prio[i] = o["cost"] + (1800 + o["lat"] / BW if o["lat"] else 0) + LAT + max([prio[s] for s in succ[i]], default=0.0)
+    prio = [1e9 - i if ops[i]["kind"] == "load" else prio[i] + noise[i] for i in range(n)]
+    users = {}
+    for i, o in enumerate(ops):
+        if o["pi"]:
+            users.setdefault(o["pi"], []).append(i)
+    need = {i: {d for u in users[o["po"]] for d in ops[u]["deps"]} - {i} for i, o in enumerate(ops) if o["po"]}
+    fin, free, dmafree, at = [None] * n, {}, [0.0], [0.0] * n
+    left = [len(o["deps"]) for o in ops]
+    ready = {i for i in range(n) if not left[i]}
+    holder = [None] * 8
+    order, banks, extra, pick = [], {}, {}, [0] * n
+    while ready:
+        cand = []
+        fb = [(max([fin[u] for u in users[h]]) if h else 0.0, k) for k, h in enumerate(holder)
+              if h is None or all(fin[u] is not None for u in users[h])]
+        tb, b = min(fb) if fb else (0.0, None)
+        for i in ready:
+            o = ops[i]
+            t = at[i]
+            if o["po"]:
+                if not fb or any(fin[d] is None for d in need[i]):
+                    continue
+                t = max(t, tb)
+            e, c, _ = o["opts"][0]
+            x, t0 = 0, max(t, free.get(e, 0.0))
+            if len(o["opts"]) > 1:
+                e1, c1, _ = o["opts"][1]
+                t1 = max(t, free.get(e1, 0.0))
+                if t1 + c1 + (bias[i] if e1 == "dve" else -bias[i]) < t0 + c:
+                    x, t0, e = 1, t1, e1
+            cand.append((t0, i, x, e))
+        t0, _, _, e = min(cand)
+        t, i, x, e = max([c for c in cand if c[3] == e and c[0] <= t0 + eps], key=lambda c: prio[c[1]])
+        o = ops[i]
+        pick[i] = x
+        if o["po"]:
+            if holder[b]:
+                extra[i] = list(users[holder[b]])
+            holder[b] = o["po"]
+            banks[o["po"]] = b
+        end = t + o["opts"][x][1]
+        if e != "recv":
+            free[e] = end
+        if o["lat"]:
+            end = dma_end(o, end, dmafree)
+        fin[i] = end + (LAT if e != "recv" else 0)
+        order.append(i)
+        ready.discard(i)
+        for s in succ[i]:
+            left[s] -= 1
+            at[s] = max(at[s], fin[i])
+            if not left[s]:
+                ready.add(s)
+    assert len(order) == n
+    return order, banks, extra, fin, pick
+
+
+def replay(ops, plan, pe, ga, sc, lat):
+    order, _, extra, _, pick = plan
+    fin, free, dmafree = {}, {}, [0.0]
+    for i in order:
+        o = ops[i]
+        e, c, _ = o["opts"][pick[i]]
+        c *= pe if e == "pe" else ga if o["kind"] == "g" else sc if o["kind"] == "s" else 1.0
+        end = max([free.get(e, 0.0)] + [fin[d] for d in o["deps"]] + [fin[d] for d in extra.get(i, ())]) + c
+        if e != "recv":
+            free[e] = end
+        fin[i] = (dma_end(o, end, dmafree) if o["lat"] else end) + (lat if e != "recv" else 0)
+    return max(fin.values())
+
+
+def best_plan(ops):
+    rng = np.random.default_rng(SEED)
+    n = len(ops)
+    best, noise, bias = None, np.zeros(n), np.full(n, 300.0)
+    for k in range(TRIES):
+        z, b = noise.copy(), bias.copy()
+        if k:
+            m = rng.random(n) < 0.02
+            z[m] = rng.normal(0, 2500, int(m.sum()))
+            m = rng.random(n) < 0.02
+            b[m] = rng.normal(300, 600, int(m.sum()))
+        p = schedule(ops, z.tolist(), b.tolist(), EPS)
+        c = [replay(ops, p, *m) for m in CASES]
+        if best is None or sum(c) <= best[0]:
+            best, noise, bias = (sum(c), p, c), z, b
+    PLAN["c"] = best[2]
+    return best[1]
+
+
+def rank_program(g, core, T, topo):
+    if T.rank_of(core) is None:
+        return
+    ops, bank = build(g, core, T, topo)
+    if "p" not in PLAN:
+        PLAN["p"] = best_plan(ops)
+    order, banks, extra, fin, pick = PLAN["p"]
+    for o, x in zip(ops, pick):
+        o["eng"], o["cost"], o["fn"] = o["opts"][x]
+    bank.update(banks)
+    queue = {"pe": g.tensor, "dve": g.vector, "act": g.scalar, "pool": g, "sync": g.sync}
+    deps = [set(o["deps"]) | set(extra.get(i, ())) for i, o in enumerate(ops)]
+    needed = set()
+    for i, d in enumerate(deps):
+        if ops[i]["eng"] != "recv":
+            needed.update(d)
+    count, known, clock, sig, sent, outs = {}, {e: {} for e in queue}, {}, {}, 0, []
+    for i in order:
+        o = ops[i]
+        e = o["eng"]
+        if e == "recv":
+            sig[i], clock[i] = o["sig"], {}
+            continue
+        kn = known[e]
+        want = {}
+        for d in deps[i]:
+            s, val = sig[d]
+            if want.get(s, (0, 0))[0] < val:
+                want[s] = (val, d)
+        for s, (val, d) in sorted(want.items(), key=lambda x: -fin[x[1][1]]):
+            if kn.get(s, 0) < val:
+                queue[e].wait_ge(T.sem[s], val)
+                kn[s] = val
+                for s2, v2 in clock[d].items():
+                    if kn.get(s2, 0) < v2:
+                        kn[s2] = v2
+        clock[i] = dict(kn)
+        r = o["fn"]()
+        if o["sig"] is None:
+            if i in needed:
+                count[e] = count.get(e, 0) + 1
+                r.then_inc(T.sem[e], 1)
+                sig[i] = (e, count[e])
+        elif o["sig"][0] == "lsem":
+            sent += o["sig"][1]
+        else:
+            r.then_inc(T.sem[o["sig"][0]], 16)
+            sig[i] = o["sig"]
+            if i not in needed:
+                outs.append(o["sig"][0])
+    g.wait_ge(T.sem.lsem, sent)
+    for s in outs:
+        g.sync.wait_ge(T.sem[s], 16)

@@ -4,24 +4,25 @@ from concourse.mybir import AluOpType as A, AxisListType, ActivationFunctionType
 P, NT, WR, H = 4096, 1536, 128, 1024
 NB = NT - WR
 TW = P + 240
-CH = [(0, 352), (352, 704), (704, 1056), (1056, 1408)]
+CH = [(0, 416), (416, 832), (832, 1184), (1184, 1408)]
 WG = [[0, 1], [2, 3]]
 LP = [0, 608, 1216, 1824, 2432, 3040, 3648, 3968, 4096]
 LC = len(LP) - 1
-HP = 3072
+HP = 3840
 SCRATCH = {
     "TP": ("sbuf", [128, TW], "int32"), "TR": ("sbuf", [128, TW], "int32"), "TB": ("sbuf", [128, TW], "int32"),
     "IOTA": ("sbuf", [128, P], "float32"), "eq": ("sbuf", [128, 48, 128], "bfloat16"),
-    "hb": ("sbuf", [128, 58600], "bfloat16"), "hf": ("sbuf", [128, 3300], "float32"),
+    "hb": ("sbuf", [128, 58600], "bfloat16"), "hf": ("sbuf", [128, 3500], "float32"),
     "hi": ("sbuf", [128, 4200], "int32"), "hh": ("sbuf", [128, 5800], "float16"), "hu": ("sbuf", [128, 800], "uint16"),
 }
 for _k in range(8):
     SCRATCH["ps%d" % _k] = ("psum", [128, 512], "float32")
 SEMAPHORES = ["pe", "dve", "act", "pool", "lsem"] + ["d%d" % _k for _k in range(24)] + ["r%d" % _k for _k in range(16)]
 ALIGN = {"hb": 8, "hf": 4, "hi": 4, "hh": 8, "hu": 8}
-CYC, GA, SC, FIX, PEC, LAT, BW = 1.0, 1.56, 3.8, 60.0, 0.5, 100.0, 200.0
-CASES = [(1, 1, 1, 100), (1, .72, .5, 60), (1, 1.28, 1.5, 200), (.8, 1, 1, 200), (1.3, 1, 1, 100)]
-TRIES, SEED, EPS = 2500, 0, 100
+CYC, GA, SC, FIX, PEC, LAT, BW = 0.95, 1.56, 3.8, 60.0, 0.477, 100.0, 200.0
+CASES = [(.88, 1, 1, 100, 400, 1300, 200), (1, .75, .6, 150, 900, 2200, 200), (1.1, 1.25, 1.4, 60, 600, 1000, 250), (1.3, 1, 1, 100, 700, 1800, 170)]
+REF = (63500, 72500, 77700, 85600)
+TRIES, SEED, EPS = 6500, 1, 30
 RC = -(2048 + 31.0 / 64)
 PLAN = {}
 
@@ -49,6 +50,8 @@ def build(g, core, T, topo):
 
     def ap(t, a=0, b=None, step=None):
         if len(t) > 4:
+            if b is not None:
+                return T[t[0]][:, t[1] + 16 * a + 15:t[1] + 16 * a + 16]
             return T[t[0]][:, t[1] + t[4]:t[1] + t[2]:16]
         b = t[2] if b is None else b
         return T[t[0]][:, t[1] + a:t[1] + b:step] if step else T[t[0]][:, t[1] + a:t[1] + b]
@@ -90,7 +93,7 @@ def build(g, core, T, topo):
         def fn():
             for k, t in enumerate(terms):
                 a, b = t[3] if len(t) > 3 else (0, w)
-                r = PE.matmul(ps(name, b, a), t[0], t[1], k == 0, k == len(terms) - 1)
+                r = PE.matmul(ps(name, b, a), t[0], t[1], k == 0 or len(t) > 4, k == len(terms) - 1 or len(terms[k + 1]) > 4)
             return r
         c = more + sum(max(64, (t[3][1] - t[3][0]) if len(t) > 3 else w) for t in terms)
         op("pe", 30 + c * PEC, [x for t in terms for x in t[2]], [], fn, ps_out=name)
@@ -199,15 +202,17 @@ def build(g, core, T, topo):
     Z16, G16 = tile("hh", 144), tile("hh", 128)
     cp(Z16, Z)
     cp(G16, G)
-    ts(cb, thi, -1024.0, -851840.0, A.mult, A.add)
-    ts(ct, thi, 4.0, 3328.0, A.mult, A.add)
+    ts(cb, thi, -1024.0, -917376.0, A.mult, A.add)
+    ts(ct, thi, 4.0, 3584.0, A.mult, A.add)
     op("dve", vc(128), [TS], [rs], lambda: V.tensor_reduce(ap(rs), ap(TS), AxisListType.X, A.add))
     ts(r1, rs, 0.0, 352.0, A.is_equal, A.mult)
     ts(gb, r1, -176.0, None, A.add)
     ts(gt, gb, -1.0 / 32, None, A.mult)
-    nI, p12I, m12I, nK, pK, I15, I25, I8K = [scaled(I, s) for s in (-1.0, 12.0, -12.0, -1024.0, 1024.0, 1.5, 2.5, 8192.0)]
+    nI, p12I, m12I, nK, pK, I15, I25 = [scaled(I, s) for s in (-1.0, 12.0, -12.0, -1024.0, 1024.0, 1.5, 2.5)]
+    I8K = scaled(I, 8192.0)
     nT64, nTK, GK = scaled(TS, -64.0), scaled(TS, -1024.0), scaled(G, 1024.0)
-    MV = B()
+    MV, MU = B(), B()
+    sel(MU, nTK, [[-1, 128]], A.not_equal, 1024.0, 0, 1)
     sel(MV, nT64, [[-1, 128]], A.not_equal, 11.0, 0, 1)
     n64f = tile("hf", 128)
     act(n64f, I, F.Identity, scale=-64.0)
@@ -227,10 +232,11 @@ def build(g, core, T, topo):
     sel(Wm, W0, [[-1, 128]], A.not_equal, -1.0, 0, 1)
     tt(M1, Wm, nT64, A.add)
     M2 = scaled(Wm, -8.0)
-    MASK, MASK6, JB = B(), B(), B()
+    MASK, JB, JC, I16 = B(), tile("hf", 128), tile("hf", 128), tile("hh", 128)
     act(MASK, mm(128, [(ap(Z, 15 - i, 143 - i), ap(INJ, 16 - i, 144 - i), [Z, INJ]) for i in range(16)]), F.Identity, 1.0 / 128, 128.0)
-    act(MASK6, MASK, F.Identity, 1.0, 6.0)
-    op("pool", 400.0, [], [JB], lambda: g.iota(ap(JB), [[16, 8], [0, 16]], 0, 1, allow_small_or_imprecise_dtypes=True))
+    cp(I16, I)
+    op("pool", 400.0, [], [JB], lambda: g.iota(ap(JB), [[16, 8], [0, 16]], 2048, 1, allow_small_or_imprecise_dtypes=True))
+    sel(JC, JB, [[0, 8], [1, 16]], A.is_equal, -4096.0, 0, 0)
     RST = scaled(sub(INJ, 0, 128), 1024.0)
     op("pool", 130 + 2 * HP * CYC, [], ["IOTA0"],
        lambda: g.iota(T.IOTA[:, 0:HP], [[1, HP]], 0, 0, allow_small_or_imprecise_dtypes=True))
@@ -250,8 +256,8 @@ def build(g, core, T, topo):
         act(d4, x, F.Identity, scale=4.0, bias=-512.0)
         for tc, ac, dc in a:
             act(ac, mm(tc[2], [(ap(I), ap(tc), [I, t]), (ap(nI), ap(dc), [nI, d4])]), F.Identity)
-    aw, dw = B(), B()
-    split(tw0, [(tw0, aw, dw)], dw)
+    ws = B(256)
+    split(tw0, [(tw0, sub(ws, 0, 128), sub(ws, 128, 256))], sub(ws, 128, 256))
     DB = [B(NB) for _ in range(3)]
     abc = chunks(B(NB))
     split(tb0, list(zip(chunks(tb0), abc, chunks(DB[0]))), DB[0])
@@ -261,20 +267,22 @@ def build(g, core, T, topo):
     def wrap(z, x, rd):
         return mm(x[2] // 16, [(ap(z, 15 - i, 143 - i), ap(x, i, x[2], 16), [z] + rd) for i in range(16)])
 
-    def pick(terms, buf):
+    def pick(terms, buf, cap=False):
         x = tile(buf, 128)
         p = mm(128, terms)
+        if cap:
+            op("dve", vc(128), [JC], [x], lambda: V.tensor_tensor_scan(ap(x), ap(JC), ps(p, 128), -4096.0, A.max, A.min), ps_in=p)
+            return x + (15,)
         op("dve", vc(128), [RST], [x], lambda: V.tensor_tensor_scan(ap(x), ap(RST), ps(p, 128), 0.0, A.add, A.max), ps_in=p)
         return x + (15,)
 
     def first_peer(d4, off, mw=None):
-        w = d4[2] // 16
-        y = tile("hi", w)
         if mw:
             x = pick([term(nK, MASK), term(Gw, d4)], "hi")
         else:
-            x = tile("hi", w)
+            x = tile("hi", d4[2] // 16)
             act(x, wrap(Zw, d4, [d4]), F.Identity)
+        y = tile("hi", d4[2] // 16)
         ts(y, x, P - 1, None, A.bitwise_and)
         cp(off, y)
         if mw:
@@ -283,8 +291,9 @@ def build(g, core, T, topo):
     def level(ga, nn):
         act(ga, mm(nn[2], [term(MV, nn)]), F.Sigmoid, scale=32.0, bias=ap(gb), rd=[gb, gt], dve=(ap(gt), None, A.is_ge))
 
-    def writers(v, j, a, d4, off, mw, an, dn, prev):
+    def writers(v, j, ws, off, mw, wn, prev):
         last = v == 2 and j == 1
+        a, d4, dn = sub(ws, 0, 128), sub(ws, 128, 256), sub(wn, 128, 256)
         be, nn, al, ad, Eb, tw, c1, db = [B() for _ in range(8)]
         Pg, E4, Pn = tile("hi", 128), tile("hi", 128), tile("hi", 128)
         gact(be, "TB", off, F.Abs, 2.5, -3.25)
@@ -296,8 +305,8 @@ def build(g, core, T, topo):
             pm = mm(128, [term(G16, se0)])
         gact(Pg, "TP", off, F.Identity, 1.0, 0.0)
         ts(E4, Pg, 60, None, A.bitwise_and)
-        act(Eb, E4, F.Identity)
-        act(ad, mm(128, [term(nI, d4), term(I, Eb)]), F.Abs)
+        act(Eb, E4, F.Identity, 1.0, -1024.0)
+        act(ad, mm(128, [term(nI, d4), term(I, Eb)]), F.Abs, bias=1024.0)
         act(nn, mm(128, [term(nI, a), term(I, be)]), F.Abs, bias=0.25)
         act(al, a, F.Abs, scale=2.5, bias=-3.25)
         s8 = 8 * (2 * v + j)
@@ -309,22 +318,20 @@ def build(g, core, T, topo):
         ptw = mm(128, [term(I, THR), (ap(GP), T.eq[:, s8:s8 + 8, 0:16], [GP] + en)]
                  + [(ap(GK), T.eq[:, s8 + c, 16:128 - 16 * c], [GK], (16 * c + 16, 128)) for c in range(7)])
         act(tw, ptw, F.Sigmoid, scale=16384.0, bias=128.0, dve=(0.0, None, A.is_ge))
-        s1, soff = tile("hf", 8), tile("hu", 8)
-        tt(s1, pick([term(nK, MASK6), term(I, JB), term(I8K, tw)], "hf"), mw, A.max)
-        ts(soff, s1, 2048.0, None, A.add)
-        act(c1, mm(128, [term(nK, a), term(pK, be), term(G, ad), term(nTK, nn), term(nK, tw)]), F.Sigmoid,
+        soff = tile("hu", 8)
+        ts(soff, pick([term(pK, MASK), term(G16, se0) if j else term(I16, Mb), term(I8K, tw)], "hf", True), 2048.0, None, A.add)
+        act(c1, mm(128, [term(MU, nn), term(G, ad), term(nK, tw)]), F.Sigmoid,
             scale=256.0, bias=ap(cb), rd=[cb, ct], dve=(ap(ct), None, A.is_ge))
         out = None
         if j == 0:
-            ga, se, off2, mw2 = B(), tile("hh", 128), tile("hu", 8), tile("hf", 8)
+            ga, se, off2 = B(), tile("hh", 128), tile("hu", 8)
             level(ga, nn)
             gtt(se, "TR", off, ga, A.mult)
             pw = pick([term(nK, MASK), term(G16, se)], "hf")
             ts(off2, pw, 2048.0, None, A.add)
-            cp(mw2, pw)
-            out = (off2, mw2, (Mb, al, se))
-        tt(an, mm(128, [term(MV, nn), term(m12I, be), term(I15, c1)]), a, A.max)
-        tt(dn, mm(128, [term(I, Eb), term(nK, ONES), term(GK, c1)]), d4, A.max)
+            out = (off2, pw, (Mb, al, se))
+        lo, hi = ((0, 128),), ((128, 256),)
+        tt(wn, mm(256, [term(MV, nn) + lo, term(m12I, be) + lo, term(I15, c1) + lo, term(I, Eb) + hi + (1,), term(GK, c1) + hi]), ws, A.max)
         act(db, mm(128, [term(nI, al), term(nTK, nn), term(pK, be), term(I25, c1)]), F.Relu, bias=2.75 - 3328.0)
         terms = [term(I, d4), term(nI, dn), term(I, db)]
         if j == 1:
@@ -363,13 +370,13 @@ def build(g, core, T, topo):
     YT, YP = B(NT), tile("hf", H)
     for v in range(3):
         offw, mww = tile("hu", 8), tile("hf", 8)
-        first_peer(dw, offw, mww)
+        first_peer(sub(ws, 128, 256), offw, mww)
         ob = tile("hu", NB // 16)
         first_peer(DB[v], ob)
         o1 = [sub(ob, s // 16, e // 16) for s, e in CH]
         bc = bulk_gather(o1)
-        a1w, d1w = B(), B()
-        off2, mw2, prev = writers(v, 0, aw, dw, offw, mww, a1w, d1w, None)
+        w1, w2 = B(256), B(256)
+        off2, mw2, prev = writers(v, 0, ws, offw, mww, w1, None)
         a1c = chunks(B(NB))
         se = tile("hh", NB)
         sec = chunks(se)
@@ -389,20 +396,23 @@ def build(g, core, T, topo):
             for k in grp:
                 o2[k] = sub(o, (CH[k][0] - s) // 16, (CH[k][1] - s) // 16)
         bc = bulk_gather(o2)
-        ws = B(256)
-        a2w, d2w = sub(ws, 0, 128, "a"), sub(ws, 128, 256, "d")
-        writers(v, 1, a1w, d1w, off2, mw2, a2w, d2w, prev)
+        writers(v, 1, w1, off2, mw2, w2, prev)
         if v < 2:
-            land = B(256)
-            send(ws, land, 1, [a2w, d2w])
-            aw, dw = sub(land, 0, 128), sub(land, 128, 256)
-            a2c, abc = chunks(B(NB)), chunks(B(NB))
+            ws = B(256)
+            send(w2, ws, 1, [w2])
+            a2, lb = B(NB), B(NB)
+            a2c, abc = chunks(a2), {}
             for k in range(len(CH)):
                 bulk_rest(bc, a1c, a2c, k)
-                send(a2c[k], abc[k], 1, [a2c[k]])
+            for grp in WG:
+                s, e = CH[grp[0]][0], CH[grp[-1]][1]
+                z = sub(lb, s, e, s)
+                send(sub(a2, s, e), z, 1, [a2c[k] for k in grp])
+                for k in grp:
+                    abc[k] = sub(z, CH[k][0] - s, CH[k][1] - s)
         else:
             y = sub(YT, 0, WR, "w")
-            tt(y, a2w, d2w, A.add)
+            act(y, mm(128, [term(I, sub(w2, 0, 128)), term(I, sub(w2, 128, 256))]), F.Identity)
             yc = chunks(YT, WR)
             for k, (s, e) in enumerate(CH):
                 bulk_rest(bc, a1c, yc, k, [(ap(I), ap(DB[v], s, e), [DB[v]])], t1[k])
@@ -416,11 +426,6 @@ def build(g, core, T, topo):
                 dma(T.yp[:, a:b], ap(yk), [yk], [], H * 256)
     PLAN["top"], PLAN["ops"] = top, ops
     return ops, bank
-
-
-def dma_end(o, end, free):
-    free[0] = max(free[0], end + 1300) + o["lat"] / BW
-    return free[0] + 500
 
 
 def schedule(ops, noise, bias, eps):
@@ -439,7 +444,7 @@ def schedule(ops, noise, bias, eps):
         if o["pi"]:
             users.setdefault(o["pi"], []).append(i)
     need = {i: {d for u in users[o["po"]] for d in ops[u]["deps"]} - {i} for i, o in enumerate(ops) if o["po"]}
-    fin, free, dmafree, at = [None] * n, {}, [0.0], [0.0] * n
+    fin, free, df, at = [None] * n, {}, 0.0, [0.0] * n
     left = [len(o["deps"]) for o in ops]
     ready = {i for i in range(n) if not left[i]}
     holder = [None] * 8
@@ -477,7 +482,8 @@ def schedule(ops, noise, bias, eps):
         if e != "recv":
             free[e] = end
         if o["lat"]:
-            end = dma_end(o, end, dmafree)
+            df = max(df, end + 1300) + o["lat"] / BW
+            end = df + 500
         fin[i] = end + (LAT if e != "recv" else 0)
         order.append(i)
         ready.discard(i)
@@ -490,18 +496,33 @@ def schedule(ops, noise, bias, eps):
     return order, banks, extra, fin, pick
 
 
-def replay(ops, plan, pe, ga, sc, lat):
+def replay(ops, plan, f, ga, sc, lat, riss, rlat, bw):
     order, _, extra, _, pick = plan
-    fin, free, dmafree = {}, {}, [0.0]
+    fin, free, df = [0.0] * len(ops), {}, 0.0
     for i in order:
         o = ops[i]
         e, c, _ = o["opts"][pick[i]]
-        c *= pe if e == "pe" else ga if o["kind"] == "g" else sc if o["kind"] == "s" else 1.0
-        end = max([free.get(e, 0.0)] + [fin[d] for d in o["deps"]] + [fin[d] for d in extra.get(i, ())]) + c
-        if e != "recv":
-            free[e] = end
-        fin[i] = (dma_end(o, end, dmafree) if o["lat"] else end) + (lat if e != "recv" else 0)
-    return max(fin.values())
+        if e == "pool" and o["lat"]:
+            c = riss
+        elif e != "sync":
+            c = c * f * (ga if o["kind"] == "g" else sc if o["kind"] == "s" else 1.0)
+        end = free.get(e, 0.0)
+        for d in o["deps"]:
+            if fin[d] > end:
+                end = fin[d]
+        for d in extra.get(i, ()):
+            if fin[d] > end:
+                end = fin[d]
+        end += c
+        if e == "recv":
+            fin[i] = end
+            continue
+        free[e] = end
+        if o["lat"]:
+            df = max(df, end + (rlat if e == "pool" else 1300)) + o["lat"] / bw
+            end = df + 500
+        fin[i] = end + lat
+    return max(fin)
 
 
 def best_plan(ops):
@@ -511,14 +532,15 @@ def best_plan(ops):
     for k in range(TRIES):
         z, b = noise.copy(), bias.copy()
         if k:
-            m = rng.random(n) < 0.02
+            m = rng.random(n) < 0.008
             z[m] = rng.normal(0, 2500, int(m.sum()))
-            m = rng.random(n) < 0.02
+            m = rng.random(n) < 0.008
             b[m] = rng.normal(300, 600, int(m.sum()))
         p = schedule(ops, z.tolist(), b.tolist(), EPS)
         c = [replay(ops, p, *m) for m in CASES]
-        if best is None or sum(c) <= best[0]:
-            best, noise, bias = (sum(c), p, c), z, b
+        c0 = sum((x / r) ** 12 for x, r in zip(c, REF))
+        if best is None or c0 <= best[0]:
+            best, noise, bias = (c0, p, c), z, b
     PLAN["c"] = best[2]
     return best[1]
 

import numpy as np
from concourse.mybir import AluOpType as A, AxisListType, ActivationFunctionType as F

P, NT, WR, H = 4096, 1536, 128, 1024
NB = NT - WR
TW = P + 240
CH = [(0, 416), (416, 832), (832, 1184), (1184, 1408)]
WG = [[0, 1], [2, 3]]
LP = [0, 608, 1216, 1824, 2432, 3040, 3648, 3968, 4096]
LC = len(LP) - 1
HP = 3840
SCRATCH = {
    "TP": ("sbuf", [128, TW], "int32"), "TR": ("sbuf", [128, TW], "int32"), "TB": ("sbuf", [128, TW], "int32"),
    "IOTA": ("sbuf", [128, P], "float32"), "eq": ("sbuf", [128, 48, 128], "bfloat16"),
    "hb": ("sbuf", [128, 58600], "bfloat16"), "hf": ("sbuf", [128, 3500], "float32"),
    "hi": ("sbuf", [128, 4200], "int32"), "hh": ("sbuf", [128, 5800], "float16"), "hu": ("sbuf", [128, 800], "uint16"),
}
for _k in range(8):
    SCRATCH["ps%d" % _k] = ("psum", [128, 512], "float32")
SEMAPHORES = ["pe", "dve", "act", "pool", "lsem"] + ["d%d" % _k for _k in range(24)] + ["r%d" % _k for _k in range(16)]
ALIGN = {"hb": 8, "hf": 4, "hi": 4, "hh": 8, "hu": 8}
CYC, GA, SC, FIX, PEC, LAT, BW = 0.95, 1.56, 3.8, 60.0, 0.477, 100.0, 200.0
CASES = [(.88, 1, 1, 100, 400, 1300, 200), (1, .75, .6, 150, 900, 2200, 200), (1.1, 1.25, 1.4, 60, 600, 1000, 250), (1.3, 1, 1, 100, 700, 1800, 170)]
REF = (63500, 72500, 77700, 85600)
TRIES, SEED, EPS = 6500, 1, 30
RC = -(2048 + 31.0 / 64)
PLAN = {}


def build(g, core, T, topo):
    ops, lastw, readers, top = [], {}, {}, {k: 0 for k in ALIGN}
    bank = {}
    cnt = {"d": 0, "r": 0, "t": 0}
    n = len(T.cores)
    rank = T.rank_of(core)
    V, S, PE = g.vector, g.scalar, g.tensor

    def tile(buf, w):
        b = top[buf]
        top[buf] = b + (w + ALIGN[buf] - 1) // ALIGN[buf] * ALIGN[buf]
        assert top[buf] <= SCRATCH[buf][1][1], (buf, top[buf])
        cnt["t"] += 1
        return (buf, b, w, "t%d" % cnt["t"])

    def sub(t, a, b, tag=None):
        return (t[0], t[1] + a, b - a, t[3] if tag is None else "%s.%s" % (t[3], tag))

    def chunks(t, o=0):
        return [sub(t, o + s, o + e, k) for k, (s, e) in enumerate(CH)]

    def ap(t, a=0, b=None, step=None):
        if len(t) > 4:
            if b is not None:
                return T[t[0]][:, t[1] + 16 * a + 15:t[1] + 16 * a + 16]
            return T[t[0]][:, t[1] + t[4]:t[1] + t[2]:16]
        b = t[2] if b is None else b
        return T[t[0]][:, t[1] + a:t[1] + b:step] if step else T[t[0]][:, t[1] + a:t[1] + b]

    def nm(x):
        return x if isinstance(x, str) else x[3]

    def op(eng, cost, rd, wr, fn, ps_in=None, ps_out=None, sig=None, after=(), lat=0.0, alt=None, kind=""):
        i = len(ops)
        deps = set(after)
        rd = [nm(x) for x in rd] + ([ps_in] if ps_in else [])
        wr = [nm(x) for x in wr] + ([ps_out] if ps_out else [])
        for x in rd:
            deps.add(lastw[x])
        for x in wr:
            if x in lastw:
                deps.add(lastw[x])
            deps.update(readers.get(x, ()))
        for x in rd:
            readers.setdefault(x, []).append(i)
        for x in wr:
            lastw[x] = i
            readers[x] = []
        deps.discard(i)
        ops.append(dict(eng=eng, cost=cost, deps=deps, fn=fn, pi=ps_in, po=ps_out, sig=sig, lat=lat, kind=kind,
                        opts=[(eng, cost, fn)] + ([alt] if alt else [])))
        return i

    def ps(name, w, a=0):
        return T["ps%d" % bank[name]][:, a:w]

    def vc(w, c=1.0):
        return FIX + max(64, w * c) * CYC

    def mm(w, terms, more=0):
        cnt["t"] += 1
        name = "p%d" % cnt["t"]

        def fn():
            for k, t in enumerate(terms):
                a, b = t[3] if len(t) > 3 else (0, w)
                r = PE.matmul(ps(name, b, a), t[0], t[1], k == 0 or len(t) > 4, k == len(terms) - 1 or len(terms[k + 1]) > 4)
            return r
        c = more + sum(max(64, (t[3][1] - t[3][0]) if len(t) > 3 else w) for t in terms)
        op("pe", 30 + c * PEC, [x for t in terms for x in t[2]], [], fn, ps_out=name)
        return name

    def term(m, x):
        return (ap(m), ap(x), [m, x])

    def act(out, src, func, scale=1.0, bias=0.0, rd=(), dve=None):
        w = out[2]
        isp = isinstance(src, str)
        if func == F.Identity:
            dve = (scale, bias, A.mult, A.add)
        if func == F.Relu:
            dve = (bias, 0.0, A.add, A.max)

        def x():
            return ps(src, w) if isp else ap(src)
        fast = 0.5 if not isp and src[0] == "hb" and out[0] == "hb" else 1.0
        alt = dve and ("dve", vc(w, fast), lambda: V.tensor_scalar(ap(out), x(), *dve))
        return op("act", vc(w), ([] if isp else [src]) + list(rd), [out],
                  lambda: S.activation(ap(out), x(), func, bias=bias, scale=scale), ps_in=src if isp else None, alt=alt)

    def ts(out, src, s1, s2, *o):
        return op("dve", vc(out[2]), [src], [out], lambda: V.tensor_scalar(ap(out), ap(src), s1, s2, *o))

    def tt(out, x, y, o):
        w = out[2]
        if isinstance(x, str):
            return op("dve", vc(w), [y], [out], lambda: V.tensor_tensor(ap(out), ps(x, w), ap(y), o), ps_in=x)
        return op("dve", vc(w, 2), [x, y], [out], lambda: V.tensor_tensor(ap(out), ap(x), ap(y), o))

    def cp(out, src):
        return op("dve", vc(out[2]), [src], [out], lambda: V.tensor_copy(ap(out), ap(src)))

    def parts(tab):
        return ["%s%d" % (tab, k) for k in range(2 if tab == "IOTA" else LC)]

    def ind(tab, off, w=P):
        return T[tab][:, 0:w].indirect(ap(off))

    def gact(out, tab, off, func, scale, bias):
        c = vc(out[2], GA)
        return op("act", c, parts(tab) + [off], [out],
                  lambda: S.activation(ap(out), ind(tab, off), func, bias=bias, scale=scale), kind="g",
                  alt=func == F.Identity and ("dve", c, lambda: V.tensor_scalar(ap(out), ind(tab, off), scale, bias, A.mult, A.add)))

    def gtt(out, tab, off, y, o):
        return op("dve", vc(out[2], GA), parts(tab) + [off, y], [out], lambda: V.tensor_tensor(ap(out), ind(tab, off), ap(y), o), kind="g")

    def scat(tab, off, src):
        return op("dve", vc(src[2], SC), [off, src], parts(tab), lambda: V.tensor_copy(ind(tab, off, TW), ap(src)), kind="s")

    def dma(out, in_, rd, wr, nbytes):
        s = "d%d" % cnt["d"]
        cnt["d"] += 1
        return op("sync", 60.0, rd, wr, lambda: g.sync.dma_start(out, in_), sig=(s, 16), lat=nbytes, kind="" if rd else "load")

    def send(src, dst, hop, rd, after=()):
        s = "r%d" % cnt["r"]
        cnt["r"] += 1
        to = T.cores[(rank + hop) % n]
        ne = len(topo.engines(T.cores[(rank - hop) % n], core))
        rid, pid, _ = topo.addr(to)
        i = op("pool", 400.0, rd, [], lambda: g.remote_dma(ap(dst), ap(src), T.sem[s], T.sem.lsem, pid, rid, topo.mask(core, to)),
               sig=("lsem", len(topo.engines(core, to))), lat=src[2] * 256, after=after)
        return op("recv", 0.0, [], [dst], None, sig=(s, ne), after=[i])

    def B(w=128):
        return tile("hb", w)

    wi, thi = tile("hi", 1), tile("hi", 1)
    trav = B(NT)
    tw0, tb0 = sub(trav, 0, WR, "w"), sub(trav, WR, NT, "b")
    dma(ap(wi), T.wts[:], [], [wi], 512)
    dma(ap(thi), T.th[:], [], [thi], 512)
    for k in range(LC):
        dma(T.TP[:, LP[k]:LP[k + 1]], T.peers[:, LP[k]:LP[k + 1]], [], ["TP%d" % k], (LP[k + 1] - LP[k]) * 512)
        if k == 0:
            dma(ap(trav), T.trav[:], [], [tw0, tb0], NT * 256)
    last_load = lastw["TP%d" % (LC - 1)]

    def fill(t, val, a=0, b=None, step=None):
        op("dve", vc(t[2] / (step or 1), 0.5), [], [t], lambda: V.memset(ap(t, a, b, step), val))

    def sel(out, src, pat, cmp, f, base, cm):
        op("pool", 170 + 2 * 128 * CYC, [src], [out], lambda: g.affine_select(ap(out), ap(src), pat, cmp, f, base, cm))

    def scaled(src, s, rd=()):
        t = B(src[2])
        act(t, src, F.Identity, scale=s, rd=rd)
        return t
    ONES, C35, g1, G, I, TS = [B() for _ in range(6)]
    fill(ONES, 1.0)
    fill(C35, 3.5)
    sel(I, ONES, [[-1, 128]], A.is_equal, 0.0, 0, 1)
    sel(g1, ONES, [[-16, 8], [0, 16]], A.is_ge, 0.0, 0, 1)
    sel(G, g1, [[16, 8], [0, 16]], A.is_ge, 0.0, 15, -1)
    sel(TS, G, [[1, 128]], A.is_gt, 0.0, 0, -1)
    Z = B(144)
    fill(Z, 0.0)
    op("dve", vc(8), [G], [Z], lambda: V.tensor_copy(ap(Z, 15, 143, 16), ap(G, 0, 128, 16)))
    wf, cb, rs, r1, gb, ct, gt = [tile("hf", 1) for _ in range(7)]
    ts(wf, wi, 0.25, None, A.mult)
    Zw, Gw = scaled(Z, ap(wf), [wf]), scaled(G, ap(wf), [wf])
    Z16, G16 = tile("hh", 144), tile("hh", 128)
    cp(Z16, Z)
    cp(G16, G)
    ts(cb, thi, -1024.0, -917376.0, A.mult, A.add)
    ts(ct, thi, 4.0, 3584.0, A.mult, A.add)
    op("dve", vc(128), [TS], [rs], lambda: V.tensor_reduce(ap(rs), ap(TS), AxisListType.X, A.add))
    ts(r1, rs, 0.0, 352.0, A.is_equal, A.mult)
    ts(gb, r1, -176.0, None, A.add)
    ts(gt, gb, -1.0 / 32, None, A.mult)
    nI, p12I, m12I, nK, pK, I15, I25 = [scaled(I, s) for s in (-1.0, 12.0, -12.0, -1024.0, 1024.0, 1.5, 2.5)]
    I8K = scaled(I, 8192.0)
    nT64, nTK, GK = scaled(TS, -64.0), scaled(TS, -1024.0), scaled(G, 1024.0)
    MV, MU = B(), B()
    sel(MU, nTK, [[-1, 128]], A.not_equal, 1024.0, 0, 1)
    sel(MV, nT64, [[-1, 128]], A.not_equal, 11.0, 0, 1)
    n64f = tile("hf", 128)
    act(n64f, I, F.Identity, scale=-64.0)
    K2, THR, GP0, GP1, Wt, W0, Wm, M1 = [B() for _ in range(8)]
    INJ = B(144)
    fill(K2, 0.5)
    fill(K2, 0.0, 0, 128, 16)
    fill(INJ, 0.0)
    fill(INJ, -1024.0, 0, 144, 16)
    op("dve", vc(128), [K2, INJ], [THR], lambda: V.tensor_tensor_scan(ap(THR), ap(K2), ap(INJ, 0, 128), 0.0, A.mult, A.add))
    tt(GP0, G, THR, A.mult)
    op("dve", vc(128), [GP0], [GP1], lambda: V.transpose(ap(GP1), ap(GP0)))
    GP = scaled(GP1, -0.5)
    K32 = scaled(K2, 1.0 / 16)
    op("dve", vc(128), [K32, I], [Wt], lambda: V.tensor_tensor_scan(ap(Wt), ap(K32), ap(I), 0.0, A.mult, A.add))
    op("dve", vc(128), [Wt], [W0], lambda: V.transpose(ap(W0), ap(Wt)))
    sel(Wm, W0, [[-1, 128]], A.not_equal, -1.0, 0, 1)
    tt(M1, Wm, nT64, A.add)
    M2 = scaled(Wm, -8.0)
    MASK, JB, JC, I16 = B(), tile("hf", 128), tile("hf", 128), tile("hh", 128)
    act(MASK, mm(128, [(ap(Z, 15 - i, 143 - i), ap(INJ, 16 - i, 144 - i), [Z, INJ]) for i in range(16)]), F.Identity, 1.0 / 128, 128.0)
    cp(I16, I)
    op("pool", 400.0, [], [JB], lambda: g.iota(ap(JB), [[16, 8], [0, 16]], 2048, 1, allow_small_or_imprecise_dtypes=True))
    sel(JC, JB, [[0, 8], [1, 16]], A.is_equal, -4096.0, 0, 0)
    RST = scaled(sub(INJ, 0, 128), 1024.0)
    op("pool", 130 + 2 * HP * CYC, [], ["IOTA0"],
       lambda: g.iota(T.IOTA[:, 0:HP], [[1, HP]], 0, 0, allow_small_or_imprecise_dtypes=True))
    op("act", vc(P - HP), ["IOTA0"], ["IOTA1"], lambda: S.activation(T.IOTA[:, HP:P], T.IOTA[:, 0:P - HP], F.Identity, bias=float(HP), scale=1.0),
       alt=("dve", vc(P - HP), lambda: V.tensor_scalar(T.IOTA[:, HP:P], T.IOTA[:, 0:P - HP], float(HP), None, A.add)))

    for k in range(LC):
        tp, tr, tb = [T[x][:, LP[k]:LP[k + 1]] for x in ("TP", "TR", "TB")]
        c = vc(LP[k + 1] - LP[k])
        op("dve", c, ["TP%d" % k], ["TB%d" % k], lambda tp=tp, tb=tb: V.tensor_scalar(tb, tp, 3, None, A.bitwise_and))
        op("act", c, ["TP%d" % k], ["TR%d" % k], lambda tp=tp, tr=tr: S.activation(tr, tp, F.Identity, bias=RC, scale=1.0 / 64),
           alt=("dve", c, lambda tp=tp, tr=tr: V.tensor_scalar(tr, tp, 1.0 / 64, RC, A.mult, A.add)))

    def split(t, a, d4):
        x = B(t[2])
        act(x, t, F.Identity, scale=0.25, bias=127.75)
        act(d4, x, F.Identity, scale=4.0, bias=-512.0)
        for tc, ac, dc in a:
            act(ac, mm(tc[2], [(ap(I), ap(tc), [I, t]), (ap(nI), ap(dc), [nI, d4])]), F.Identity)
    ws = B(256)
    split(tw0, [(tw0, sub(ws, 0, 128), sub(ws, 128, 256))], sub(ws, 128, 256))
    DB = [B(NB) for _ in range(3)]
    abc = chunks(B(NB))
    split(tb0, list(zip(chunks(tb0), abc, chunks(DB[0]))), DB[0])
    for hop in (1, 2):
        send(DB[0], DB[hop], hop, [DB[0]], [last_load])

    def wrap(z, x, rd):
        return mm(x[2] // 16, [(ap(z, 15 - i, 143 - i), ap(x, i, x[2], 16), [z] + rd) for i in range(16)])

    def pick(terms, buf, cap=False):
        x = tile(buf, 128)
        p = mm(128, terms)
        if cap:
            op("dve", vc(128), [JC], [x], lambda: V.tensor_tensor_scan(ap(x), ap(JC), ps(p, 128), -4096.0, A.max, A.min), ps_in=p)
            return x + (15,)
        op("dve", vc(128), [RST], [x], lambda: V.tensor_tensor_scan(ap(x), ap(RST), ps(p, 128), 0.0, A.add, A.max), ps_in=p)
        return x + (15,)

    def first_peer(d4, off, mw=None):
        if mw:
            x = pick([term(nK, MASK), term(Gw, d4)], "hi")
        else:
            x = tile("hi", d4[2] // 16)
            act(x, wrap(Zw, d4, [d4]), F.Identity)
        y = tile("hi", d4[2] // 16)
        ts(y, x, P - 1, None, A.bitwise_and)
        cp(off, y)
        if mw:
            act(mw, y, F.Identity, 1.0, -2048.0)

    def level(ga, nn):
        act(ga, mm(nn[2], [term(MV, nn)]), F.Sigmoid, scale=32.0, bias=ap(gb), rd=[gb, gt], dve=(ap(gt), None, A.is_ge))

    def writers(v, j, ws, off, mw, wn, prev):
        last = v == 2 and j == 1
        a, d4, dn = sub(ws, 0, 128), sub(ws, 128, 256), sub(wn, 128, 256)
        be, nn, al, ad, Eb, tw, c1, db = [B() for _ in range(8)]
        Pg, E4, Pn = tile("hi", 128), tile("hi", 128), tile("hi", 128)
        gact(be, "TB", off, F.Abs, 2.5, -3.25)
        if j == 0:
            Mb = tile("hh", 128)
            gact(Mb, "IOTA", off, F.Identity, 1.0, -2048.0)
        else:
            M0, al0, se0 = prev
            pm = mm(128, [term(G16, se0)])
        gact(Pg, "TP", off, F.Identity, 1.0, 0.0)
        ts(E4, Pg, 60, None, A.bitwise_and)
        act(Eb, E4, F.Identity, 1.0, -1024.0)
        act(ad, mm(128, [term(nI, d4), term(I, Eb)]), F.Abs, bias=1024.0)
        act(nn, mm(128, [term(nI, a), term(I, be)]), F.Abs, bias=0.25)
        act(al, a, F.Abs, scale=2.5, bias=-3.25)
        s8 = 8 * (2 * v + j)
        en = ["eq%d" % (s8 + c) for c in range(8)]
        for c in range(8):
            op("dve", vc(128 - 16 * c, 1.0 if j else 0.5), [mw] + ([] if j else [Mb]), [en[c]], lambda c=c: V.tensor_scalar(
                T.eq[:, s8 + c, 0:128 - 16 * c], ps(pm, 128, 16 * c) if j else ap(Mb, 16 * c, 128),
                ap(mw, c, c + 1), None, A.is_equal), ps_in=pm if j else None)
        ptw = mm(128, [term(I, THR), (ap(GP), T.eq[:, s8:s8 + 8, 0:16], [GP] + en)]
                 + [(ap(GK), T.eq[:, s8 + c, 16:128 - 16 * c], [GK], (16 * c + 16, 128)) for c in range(7)])
        act(tw, ptw, F.Sigmoid, scale=16384.0, bias=128.0, dve=(0.0, None, A.is_ge))
        soff = tile("hu", 8)
        ts(soff, pick([term(pK, MASK), term(G16, se0) if j else term(I16, Mb), term(I8K, tw)], "hf", True), 2048.0, None, A.add)
        act(c1, mm(128, [term(MU, nn), term(G, ad), term(nK, tw)]), F.Sigmoid,
            scale=256.0, bias=ap(cb), rd=[cb, ct], dve=(ap(ct), None, A.is_ge))
        out = None
        if j == 0:
            ga, se, off2 = B(), tile("hh", 128), tile("hu", 8)
            level(ga, nn)
            gtt(se, "TR", off, ga, A.mult)
            pw = pick([term(nK, MASK), term(G16, se)], "hf")
            ts(off2, pw, 2048.0, None, A.add)
            out = (off2, pw, (Mb, al, se))
        lo, hi = ((0, 128),), ((128, 256),)
        tt(wn, mm(256, [term(MV, nn) + lo, term(m12I, be) + lo, term(I15, c1) + lo, term(I, Eb) + hi + (1,), term(GK, c1) + hi]), ws, A.max)
        act(db, mm(128, [term(nI, al), term(nTK, nn), term(pK, be), term(I25, c1)]), F.Relu, bias=2.75 - 3328.0)
        terms = [term(I, d4), term(nI, dn), term(I, db)]
        if j == 1:
            bad, sw, dm, sd = B(), B(), tile("hf", 128), tile("hf", 128)
            act(bad, mm(128, [term(I, al), term(I, be)]), F.Relu, bias=-3.5)
            act(sw, mm(128, [term(m12I, C35), term(p12I, al0), term(p12I, a), term(m12I, al), term(M1, nn), term(M2, bad)]),
                F.Sigmoid, scale=2.0 ** 84, bias=-100.0, dve=(0.0, None, A.is_gt))
            gtt(dm, "TR", off, M0, A.subtract)
            tt(sd, dm, sw, A.mult)
            terms = [term(n64f, sd)] + terms
        tt(Pn, mm(128, terms, 384 * j), Pg, A.add)
        if not last:
            bn = tile("hi", 128)
            ts(bn, Pn, 3, None, A.bitwise_and)
            scat("TB", soff, bn)
        scat("TP", soff, Pn)
        if j == 1 and not last:
            rn = tile("hi", 128)
            act(rn, Pn, F.Identity, 1.0 / 64, RC)
            scat("TR", soff, rn)
        return out

    def bulk_gather(offs):
        bc = chunks(B(NB))
        for k in range(len(CH)):
            gact(bc[k], "TB", offs[k], F.Abs, 2.5, -3.25)
        return bc

    def bulk_rest(bc, a, an, k, extra=(), base=None):
        nn = B(bc[k][2])
        w = nn[2]
        act(nn, mm(w, [term(nI, a[k]), term(I, bc[k])]), F.Abs, bias=0.25)
        tt(an[k], mm(w, list(extra) + [term(m12I, bc[k]), term(MV, nn)]), base or a[k], A.max)
        return nn

    YT, YP = B(NT), tile("hf", H)
    for v in range(3):
        offw, mww = tile("hu", 8), tile("hf", 8)
        first_peer(sub(ws, 128, 256), offw, mww)
        ob = tile("hu", NB // 16)
        first_peer(DB[v], ob)
        o1 = [sub(ob, s // 16, e // 16) for s, e in CH]
        bc = bulk_gather(o1)
        w1, w2 = B(256), B(256)
        off2, mw2, prev = writers(v, 0, ws, offw, mww, w1, None)
        a1c = chunks(B(NB))
        se = tile("hh", NB)
        sec = chunks(se)
        t1 = chunks(B(NB)) if v == 2 else None
        for k, (s, e) in enumerate(CH):
            ga = B(e - s)
            level(ga, bulk_rest(bc, abc, a1c, k))
            gtt(sec[k], "TR", o1[k], ga, A.mult)
            if v == 2:
                act(t1[k], mm(e - s, [(ap(I), ap(DB[v], s, e), [DB[v]]), term(I, a1c[k])]), F.Identity)
        o2 = {}
        for grp in WG:
            s, e = CH[grp[0]][0], CH[grp[-1]][1]
            o = tile("hu", (e - s) // 16)
            p = wrap(Z16, sub(se, s, e), [sec[k] for k in grp])
            op("dve", vc(o[2]), [], [o], lambda o=o, p=p: V.tensor_scalar(ap(o), ps(p, o[2]), 2048.0, None, A.add), ps_in=p)
            for k in grp:
                o2[k] = sub(o, (CH[k][0] - s) // 16, (CH[k][1] - s) // 16)
        bc = bulk_gather(o2)
        writers(v, 1, w1, off2, mw2, w2, prev)
        if v < 2:
            ws = B(256)
            send(w2, ws, 1, [w2])
            a2, lb = B(NB), B(NB)
            a2c, abc = chunks(a2), {}
            for k in range(len(CH)):
                bulk_rest(bc, a1c, a2c, k)
            for grp in WG:
                s, e = CH[grp[0]][0], CH[grp[-1]][1]
                z = sub(lb, s, e, s)
                send(sub(a2, s, e), z, 1, [a2c[k] for k in grp])
                for k in grp:
                    abc[k] = sub(z, CH[k][0] - s, CH[k][1] - s)
        else:
            y = sub(YT, 0, WR, "w")
            act(y, mm(128, [term(I, sub(w2, 0, 128)), term(I, sub(w2, 128, 256))]), F.Identity)
            yc = chunks(YT, WR)
            for k, (s, e) in enumerate(CH):
                bulk_rest(bc, a1c, yc, k, [(ap(I), ap(DB[v], s, e), [DB[v]])], t1[k])
                dma(T.yt[:, WR + s:WR + e], ap(yc[k]), [yc[k]], [], (e - s) * 256)
            dma(T.yt[:, 0:WR], ap(y), [y], [], WR * 256)
            for k in range(2):
                a, b = k * H // 2, (k + 1) * H // 2
                yk = sub(YP, a, b, k)
                op("dve", vc(H // 2), parts("TP"), [yk], lambda a=a, b=b, yk=yk: V.tensor_copy(ap(yk), T.TP[:, a:b]),
                   alt=("act", vc(H // 2), lambda a=a, b=b, yk=yk: S.activation(ap(yk), T.TP[:, a:b], F.Identity)))
                dma(T.yp[:, a:b], ap(yk), [yk], [], H * 256)
    PLAN["top"], PLAN["ops"] = top, ops
    return ops, bank


def schedule(ops, noise, bias, eps):
    n = len(ops)
    succ = [[] for _ in ops]
    for i, o in enumerate(ops):
        for d in o["deps"]:
            succ[d].append(i)
    prio = [0.0] * n
    for i in range(n - 1, -1, -1):
        o = ops[i]
        prio[i] = o["cost"] + (1800 + o["lat"] / BW if o["lat"] else 0) + LAT + max([prio[s] for s in succ[i]], default=0.0)
    prio = [1e9 - i if ops[i]["kind"] == "load" else prio[i] + noise[i] for i in range(n)]
    users = {}
    for i, o in enumerate(ops):
        if o["pi"]:
            users.setdefault(o["pi"], []).append(i)
    need = {i: {d for u in users[o["po"]] for d in ops[u]["deps"]} - {i} for i, o in enumerate(ops) if o["po"]}
    fin, free, df, at = [None] * n, {}, 0.0, [0.0] * n
    left = [len(o["deps"]) for o in ops]
    ready = {i for i in range(n) if not left[i]}
    holder = [None] * 8
    order, banks, extra, pick = [], {}, {}, [0] * n
    while ready:
        cand = []
        fb = [(max([fin[u] for u in users[h]]) if h else 0.0, k) for k, h in enumerate(holder)
              if h is None or all(fin[u] is not None for u in users[h])]
        tb, b = min(fb) if fb else (0.0, None)
        for i in ready:
            o = ops[i]
            t = at[i]
            if o["po"]:
                if not fb or any(fin[d] is None for d in need[i]):
                    continue
                t = max(t, tb)
            e, c, _ = o["opts"][0]
            x, t0 = 0, max(t, free.get(e, 0.0))
            if len(o["opts"]) > 1:
                e1, c1, _ = o["opts"][1]
                t1 = max(t, free.get(e1, 0.0))
                if t1 + c1 + (bias[i] if e1 == "dve" else -bias[i]) < t0 + c:
                    x, t0, e = 1, t1, e1
            cand.append((t0, i, x, e))
        t0, _, _, e = min(cand)
        t, i, x, e = max([c for c in cand if c[3] == e and c[0] <= t0 + eps], key=lambda c: prio[c[1]])
        o = ops[i]
        pick[i] = x
        if o["po"]:
            if holder[b]:
                extra[i] = list(users[holder[b]])
            holder[b] = o["po"]
            banks[o["po"]] = b
        end = t + o["opts"][x][1]
        if e != "recv":
            free[e] = end
        if o["lat"]:
            df = max(df, end + 1300) + o["lat"] / BW
            end = df + 500
        fin[i] = end + (LAT if e != "recv" else 0)
        order.append(i)
        ready.discard(i)
        for s in succ[i]:
            left[s] -= 1
            at[s] = max(at[s], fin[i])
            if not left[s]:
                ready.add(s)
    assert len(order) == n
    return order, banks, extra, fin, pick


def replay(ops, plan, f, ga, sc, lat, riss, rlat, bw):
    order, _, extra, _, pick = plan
    fin, free, df = [0.0] * len(ops), {}, 0.0
    for i in order:
        o = ops[i]
        e, c, _ = o["opts"][pick[i]]
        if e == "pool" and o["lat"]:
            c = riss
        elif e != "sync":
            c = c * f * (ga if o["kind"] == "g" else sc if o["kind"] == "s" else 1.0)
        end = free.get(e, 0.0)
        for d in o["deps"]:
            if fin[d] > end:
                end = fin[d]
        for d in extra.get(i, ()):
            if fin[d] > end:
                end = fin[d]
        end += c
        if e == "recv":
            fin[i] = end
            continue
        free[e] = end
        if o["lat"]:
            df = max(df, end + (rlat if e == "pool" else 1300)) + o["lat"] / bw
            end = df + 500
        fin[i] = end + lat
    return max(fin)


def best_plan(ops):
    rng = np.random.default_rng(SEED)
    n = len(ops)
    best, noise, bias = None, np.zeros(n), np.full(n, 300.0)
    for k in range(TRIES):
        z, b = noise.copy(), bias.copy()
        if k:
            m = rng.random(n) < 0.008
            z[m] = rng.normal(0, 2500, int(m.sum()))
            m = rng.random(n) < 0.008
            b[m] = rng.normal(300, 600, int(m.sum()))
        p = schedule(ops, z.tolist(), b.tolist(), EPS)
        c = [replay(ops, p, *m) for m in CASES]
        c0 = sum((x / r) ** 12 for x, r in zip(c, REF))
        if best is None or c0 <= best[0]:
            best, noise, bias = (c0, p, c), z, b
    PLAN["c"] = best[2]
    return best[1]


def rank_program(g, core, T, topo):
    if T.rank_of(core) is None:
        return
    ops, bank = build(g, core, T, topo)
    if "p" not in PLAN:
        PLAN["p"] = best_plan(ops)
    order, banks, extra, fin, pick = PLAN["p"]
    for o, x in zip(ops, pick):
        o["eng"], o["cost"], o["fn"] = o["opts"][x]
    bank.update(banks)
    queue = {"pe": g.tensor, "dve": g.vector, "act": g.scalar, "pool": g, "sync": g.sync}
    deps = [set(o["deps"]) | set(extra.get(i, ())) for i, o in enumerate(ops)]
    needed = set()
    for i, d in enumerate(deps):
        if ops[i]["eng"] != "recv":
            needed.update(d)
    count, known, clock, sig, sent, outs = {}, {e: {} for e in queue}, {}, {}, 0, []
    for i in order:
        o = ops[i]
        e = o["eng"]
        if e == "recv":
            sig[i], clock[i] = o["sig"], {}
            continue
        kn = known[e]
        want = {}
        for d in deps[i]:
            s, val = sig[d]
            if want.get(s, (0, 0))[0] < val:
                want[s] = (val, d)
        for s, (val, d) in sorted(want.items(), key=lambda x: -fin[x[1][1]]):
            if kn.get(s, 0) < val:
                queue[e].wait_ge(T.sem[s], val)
                kn[s] = val
                for s2, v2 in clock[d].items():
                    if kn.get(s2, 0) < v2:
                        kn[s2] = v2
        clock[i] = dict(kn)
        r = o["fn"]()
        if o["sig"] is None:
            if i in needed:
                count[e] = count.get(e, 0) + 1
                r.then_inc(T.sem[e], 1)
                sig[i] = (e, count[e])
        elif o["sig"][0] == "lsem":
            sent += o["sig"][1]
        else:
            r.then_inc(T.sem[o["sig"][0]], 16)
            sig[i] = o["sig"]
            if i not in needed:
                outs.append(o["sig"][0])
    g.wait_ge(T.sem.lsem, sent)
    for s in outs:
        g.sync.wait_ge(T.sem[s], 16)
